import numpy as np
import ml_dtypes


def mxq(x, axis, fmt="e4m3"):
    dtype, down = {"e4m3": (ml_dtypes.float8_e4m3fn, 7), "e5m2": (ml_dtypes.float8_e5m2, 14)}[fmt]
    v = np.moveaxis(np.asarray(x, np.float32).astype(ml_dtypes.bfloat16).astype(np.float64), axis, -1)
    blocks = v.reshape(v.shape[:-1] + (-1, 32))
    amax = np.abs(blocks).max(-1, keepdims=True)
    byte = np.maximum(np.where(amax > 0, np.frexp(amax)[1] - 1 + 127, 0) - down, 1)
    scale = np.exp2(byte - 127.0)
    codes = (blocks / scale).astype(np.float32).astype(dtype).astype(np.float64)
    return np.moveaxis((codes * scale).reshape(v.shape), -1, axis)


WIDE = False


def mx_kscale(k):
    if not WIDE:
        return np.ones(k)
    levels = np.array([10, -10, 5, -5, 0])
    if k % 512:
        return np.exp2(np.random.permutation(np.resize(levels, k // 32))).repeat(32)
    a = np.empty((k // 512, 16))
    for p in range(k // 512):
        a[p, :8] = np.random.permutation(np.resize(levels, 8))
        for g in range(8):
            far = levels[np.abs(levels - a[p, g]) >= 10]
            a[p, g + 8] = far[np.random.randint(len(far))]
    return np.exp2(a.ravel()).repeat(32)


def f64(x):
    return np.asarray(x).astype(np.float64)


def striped(idx):
    return np.tile(idx.reshape(-1, 16).T, (8, 1)).astype(np.uint16)


def unstriped(offs):
    return offs[:16].T.reshape(-1).astype(np.int64)


def striped8(idx):
    return np.concatenate([x.reshape(-1, 16).T for x in idx]).astype(np.uint16)


def runs(offs, k):
    lists = np.stack([offs[16 * r : 16 * r + 16].T.reshape(-1) for r in range(8)]).astype(np.int64)
    return lists[np.arange(k) % 512 // 64]


def pack_weight(w):
    k, n = w.shape
    w = f64(np.asarray(w, np.float32).astype(ml_dtypes.bfloat16)).reshape(k // 32, 32, n)
    amax = np.abs(w).max(1)
    byte = np.clip(np.where(amax > 0, np.frexp(amax)[1] - 1 + 127 - 7, 1), 1, 254)
    scaled = (w * np.exp2(127.0 - byte)[:, None, :]).reshape(k, n).astype(np.float32)
    words = np.ascontiguousarray(scaled.reshape(k // 512, 128, 4, n).transpose(0, 1, 3, 2)).astype(ml_dtypes.float8_e4m3fn).view(np.uint8)
    return words, np.ascontiguousarray(byte.astype(np.uint8).reshape(k // 512, 16, n))


def unpack_weight(words, scales):
    g, p, n, _ = words.shape
    vals = np.ascontiguousarray(words).view(ml_dtypes.float8_e4m3fn).astype(np.float64) * np.repeat(np.exp2(scales.astype(np.float64) - 127.0), 8, axis=1)[..., None]
    return vals.transpose(0, 1, 3, 2).reshape(g * 512, n)


K, T, S, N, H, J = 512, 2048, 512, 512, 512, 512


def setup_inputs():
    n = np.random.standard_normal
    s = mx_kscale(K)[:, None]
    u = mx_kscale(H)
    packed_xT = pack_weight(n((K, T)) * s)
    return {
        "x_words": packed_xT[0],
        "x_scales": packed_xT[1],
        "w1": (n((K, H)) / np.sqrt(K) / s).astype(np.float32),
        "tab": n((H, J)).astype(np.float32),
        "gn": (np.random.uniform(0.5, 1.5, (H, 1)) * u[:, None]).astype(np.float32),
        "w2": (n((H, N)) / np.sqrt(H) / u[:, None]).astype(np.float32),
        "offs": striped(np.random.permutation(T)[:S]),
        "n1": striped8(np.random.randint(0, J, (8, S))),
        "n2": striped8(np.stack([np.random.permutation(S) for _ in range(8)])),
        "n3": striped8(np.stack([np.random.permutation(S) for _ in range(8)])),
        "n4": striped8(np.stack([np.random.permutation(S) for _ in range(8)])),
    }


def reference(x_words, x_scales, w1, tab, gn, w2, offs, n1, n2, n3, n4):
    xq = unpack_weight(x_words, x_scales)[:, unstriped(offs)]
    y = mxq(f64(w1), 0, "e4m3").T @ xq
    z = f64(gn) * (np.maximum(y + f64(tab)[np.arange(H)[:, None], runs(n1, H)], y[np.arange(H)[:, None], runs(n2, H)]))
    h = mxq(f64(w2), 0, "e4m3").T @ mxq(z, 0, "e4m3")
    st = h - (h[np.arange(N)[:, None], runs(n3, N)])
    return np.maximum(st, st[np.arange(N)[:, None], runs(n4, N)])

@@ -1,0 +1,169 @@
+from contextlib import ExitStack
+
+import concourse.mybir as mybir
+
+K, T, S, N, H, J = 512, 2048, 512, 512, 512, 512
+FLOPS = 2 * K * H * S + 2 * H * N * S
+
+F32 = mybir.dt.float32
+BF16 = mybir.dt.bfloat16
+I32 = mybir.dt.int32
+U32 = mybir.dt.uint32
+U16 = mybir.dt.uint16
+U8 = mybir.dt.uint8
+FP8X4 = mybir.dt.float8_e4m3fn_x4
+ALU = mybir.AluOpType
+COPY = mybir.ActivationFunctionType.Copy
+
+P = 128
+PACK = 4
+STRIPE = 16
+W1_SPLIT = 80
+HALVES = [(0, 256), (256, 512)]
+Z_CHUNKS = [(0, 256), (256, 384), (384, 512)]
+
+
+def tile_picked_laykindhopmx_none_p_kernel(
+    tc, x_words, x_scales, w1, tab, gn, w2, offs, n1, n2, n3, n4, out
+):
+    nc = tc.nc
+    with ExitStack() as ctx:
+        keep = ctx.enter_context(tc.tile_pool(name="keep", bufs=1))
+        psum = ctx.enter_context(tc.psum_pool(name="psum", bufs=1))
+
+        def load_list(name, dram):
+            held = keep.tile([P, S // STRIPE], U16, name=name)
+            nc.sync.dma_start(held[:], dram)
+            return held
+
+        def entries(held, lo, hi):
+            return held[:, lo // STRIPE : hi // STRIPE]
+
+        def rows(name, width, dtype=F32):
+            return [keep.tile([P, width], dtype, name=f"{name}{t}", align_bytes=64) for t in range(PACK)]
+
+        xs = keep.tile([P, T], U8, name="xs", align_bytes=64)
+        nc.vector.memset(xs[:].bitcast(I32), 0)
+        w1_raw = keep.tile([P, PACK, H], F32, name="w1_raw")
+        nc.sync.dma_start(w1_raw[:], w1.rearrange("(p j) c -> p j c", j=PACK))
+        for q in range(4):
+            nc.sync.dma_start(xs[32 * q : 32 * q + 4, :].bitcast(I32), x_scales[0, 4 * q : 4 * q + 4, :].bitcast(I32))
+        offs_l = load_list("offs_l", offs)
+        xw = keep.tile([P, T], U32, name="xw", align_bytes=64)
+        nc.sync.dma_start(xw[:].bitcast(I32), x_words[0].rearrange("p n r -> p (n r)").bitcast(I32))
+        n1_l = load_list("n1_l", n1)
+        tab_rows = tab.rearrange("(p t) c -> p t c", t=PACK)
+        tab_w = rows("tab_w", J)
+        w2_rows = w2.rearrange("(p j) c -> p j c", j=PACK)
+        w2_raw = [keep.tile([P, PACK, N // 2], F32, name=f"w2_raw{u}") for u in range(2)]
+        nc.sync.dma_start(tab_w[0][:], tab_rows[:, 0, :])
+        nc.sync.dma_start(tab_w[1][:], tab_rows[:, 1, :])
+        n2_l = load_list("n2_l", n2)
+        nc.sync.dma_start(w2_raw[0][:], w2_rows[:, :, 0 : N // 2])
+        nc.sync.dma_start(tab_w[2][:], tab_rows[:, 2, :])
+        nc.sync.dma_start(tab_w[3][:], tab_rows[:, 3, :])
+        nc.sync.dma_start(w2_raw[1][:], w2_rows[:, :, N // 2 : N])
+        gain = keep.tile([P, PACK], F32, name="gain")
+        nc.sync.dma_start(gain[:], gn.rearrange("(p t) o -> p (t o)", t=PACK))
+        n3_l = load_list("n3_l", n3)
+        n4_l = load_list("n4_l", n4)
+
+        w1_grp = keep.tile([P, PACK, P, PACK], BF16, name="w1_grp", align_bytes=64)
+        w1_src = w1_raw[:].rearrange("p j (m t) -> p m j t", t=PACK)
+        w1_dst = w1_grp[:].rearrange("p t m j -> p m j t")
+        nc.vector.tensor_copy(w1_dst[:, 0:W1_SPLIT], w1_src[:, 0:W1_SPLIT])
+        nc.scalar.copy(w1_dst[:, W1_SPLIT:P], w1_src[:, W1_SPLIT:P])
+
+        xs_g = keep.tile([P, S], U8, name="xs_g", align_bytes=64)
+        nc.vector.tensor_copy(xs_g[:], xs[:].indirect(offs_l[:]))
+        w1_q = keep.tile([P, H], U32, name="w1_q", align_bytes=64)
+        w1_s = keep.tile([P, H], U8, name="w1_s", align_bytes=64)
+        nc.vector.quantize_mx(w1_q[:].bitcast(FP8X4), w1_s[:], w1_grp[:].rearrange("p t m j -> p (t m j)"))
+
+        xw_g = [keep.tile([P, hi - lo], U32, name=f"xw_g{lo}", align_bytes=64) for lo, hi in HALVES]
+        for u, (lo, hi) in enumerate(HALVES):
+            nc.vector.tensor_copy(xw_g[u][:], xw[:].indirect(entries(offs_l, lo, hi)))
+
+        y_ps = [psum.tile([P, S], F32, name=f"y_ps{t}") for t in range(PACK)]
+        y_w = rows("y_w", S)
+        for u, (lo, hi) in enumerate(HALVES):
+            for t in range(PACK):
+                cols = slice(t * P, (t + 1) * P)
+                nc.tensor.matmul_mx(
+                    out=y_ps[t][:, lo:hi],
+                    lhsT=w1_q[:, cols].bitcast(FP8X4),
+                    lhsT_scale=w1_s[:, cols],
+                    rhs=xw_g[u][:].bitcast(FP8X4),
+                    rhs_scale=xs_g[:, lo:hi],
+                    start=True,
+                    stop=True,
+                )
+                nc.scalar.copy(y_w[t][:, lo:hi], y_ps[t][:, lo:hi])
+
+        first = rows("first", S)
+        for lo, hi in HALVES:
+            for t in range(PACK):
+                nc.vector.tensor_tensor(first[t][:, lo:hi], tab_w[t][:].indirect(entries(n1_l, lo, hi)), y_w[t][:, lo:hi], ALU.add)
+
+        w2_grp = keep.tile([P, PACK, P, PACK], BF16, name="w2_grp", align_bytes=64)
+        for u in range(2):
+            nc.scalar.copy(
+                w2_grp[:, :, u * 64 : (u + 1) * 64, :].rearrange("p t m j -> p m j t"),
+                w2_raw[u][:].rearrange("p j (m t) -> p m j t", t=PACK),
+            )
+        w2_q = keep.tile([P, N], U32, name="w2_q", align_bytes=64)
+        w2_s = keep.tile([P, N], U8, name="w2_s", align_bytes=64)
+        nc.vector.quantize_mx(w2_q[:].bitcast(FP8X4), w2_s[:], w2_grp[:].rearrange("p t m j -> p (t m j)"))
+
+        second = rows("second", S)
+        larger = rows("larger", S)
+        h_ps = [psum.tile([P, S], F32, name=f"h_ps{t}") for t in range(PACK)]
+        hneg_w = rows("hneg_w", S)
+        h_sb = rows("h_sb", S)
+        for lo, hi in Z_CHUNKS:
+            z16 = keep.tile([P, hi - lo, PACK], BF16, name=f"z16_{lo}", align_bytes=64)
+            for t in range(PACK):
+                nc.vector.tensor_copy(second[t][:, lo:hi], y_w[t][:].indirect(entries(n2_l, lo, hi)))
+                nc.vector.tensor_tensor(larger[t][:, lo:hi], first[t][:, lo:hi], second[t][:, lo:hi], ALU.max)
+                nc.scalar.activation(z16[:, :, t], larger[t][:, lo:hi], COPY, scale=gain[:, t : t + 1])
+            z_q = keep.tile([P, hi - lo], U32, name=f"z_q{lo}", align_bytes=64)
+            z_s = keep.tile([P, hi - lo], U8, name=f"z_s{lo}", align_bytes=64)
+            nc.vector.quantize_mx(z_q[:].bitcast(FP8X4), z_s[:], z16[:].rearrange("p n t -> p (n t)"))
+            for t in range(PACK):
+                cols = slice(t * P, (t + 1) * P)
+                nc.tensor.matmul_mx(
+                    out=h_ps[t][:, lo:hi],
+                    lhsT=w2_q[:, cols].bitcast(FP8X4),
+                    lhsT_scale=w2_s[:, cols],
+                    rhs=z_q[:].bitcast(FP8X4),
+                    rhs_scale=z_s[:],
+                    start=True,
+                    stop=True,
+                )
+            nc.scalar.activation(hneg_w[0][:, lo:hi], h_ps[0][:, lo:hi], COPY, scale=-1.0)
+            nc.scalar.copy(h_sb[0][:, lo:hi], h_ps[0][:, lo:hi])
+        for t in range(1, PACK):
+            nc.scalar.activation(hneg_w[t][:], h_ps[t][:], COPY, scale=-1.0)
+            nc.scalar.copy(h_sb[t][:], h_ps[t][:])
+
+        st_w = rows("st_w", S)
+        other = rows("other", S)
+        res = rows("res", S)
+        out_rows = out.rearrange("(p t) c -> p t c", t=PACK)
+
+        def step(t):
+            for lo, hi in HALVES:
+                nc.vector.tensor_tensor(st_w[t][:, lo:hi], hneg_w[t][:].indirect(entries(n3_l, lo, hi)), h_sb[t][:, lo:hi], ALU.add)
+
+        def finish(t):
+            for lo, hi in HALVES:
+                nc.vector.tensor_copy(other[t][:, lo:hi], st_w[t][:].indirect(entries(n4_l, lo, hi)))
+            for lo, hi in HALVES:
+                nc.vector.tensor_tensor(res[t][:, lo:hi], st_w[t][:, lo:hi], other[t][:, lo:hi], ALU.max)
+                nc.sync.dma_start(out_rows[:, t, lo:hi], res[t][:, lo:hi])
+
+        step(0)
+        for t in range(1, PACK):
+            step(t)
+            finish(t - 1)
+        finish(PACK - 1)

@@ -53,117 +53,151 @@ def tile_picked_laykindhopmx_none_p_kernel(
         nc.sync.dma_start(xw[:].bitcast(I32), x_words[0].rearrange("p n r -> p (n r)").bitcast(I32))
         n1_l = load_list("n1_l", n1)
         tab_rows = tab.rearrange("(p t) c -> p t c", t=PACK)
-        tab_w = rows("tab_w", J)
+        tab_w = rows("tab_w", 2 * J)
+        y_w = rows("y_w", 2 * S)
+        for t in range(PACK):
+            nc.vector.memset(tab_w[t][:, J:], 0.0)
         w2_rows = w2.rearrange("(p j) c -> p j c", j=PACK)
         w2_raw = [keep.tile([P, PACK, N // 2], F32, name=f"w2_raw{u}") for u in range(2)]
-        nc.sync.dma_start(tab_w[0][:], tab_rows[:, 0, :])
-        nc.sync.dma_start(tab_w[1][:], tab_rows[:, 1, :])
+        nc.sync.dma_start(tab_w[0][:, :J], tab_rows[:, 0, :])
+        nc.sync.dma_start(tab_w[1][:, :J], tab_rows[:, 1, :])
         n2_l = load_list("n2_l", n2)
         nc.sync.dma_start(w2_raw[0][:], w2_rows[:, :, 0 : N // 2])
-        nc.sync.dma_start(tab_w[2][:], tab_rows[:, 2, :])
-        nc.sync.dma_start(tab_w[3][:], tab_rows[:, 3, :])
-        nc.sync.dma_start(w2_raw[1][:], w2_rows[:, :, N // 2 : N])
+        nc.sync.dma_start(tab_w[2][:, :J], tab_rows[:, 2, :])
         gain = keep.tile([P, PACK], F32, name="gain")
         nc.sync.dma_start(gain[:], gn.rearrange("(p t) o -> p (t o)", t=PACK))
+        nc.sync.dma_start(w2_raw[1][:], w2_rows[:, :, N // 2 : N])
+        nc.sync.dma_start(tab_w[3][:, :J], tab_rows[:, 3, :])
         n3_l = load_list("n3_l", n3)
         n4_l = load_list("n4_l", n4)
 
         w1_grp = keep.tile([P, PACK, P, PACK], BF16, name="w1_grp", align_bytes=64)
-        w1_src = w1_raw[:].rearrange("p j (m t) -> p m j t", t=PACK)
-        w1_dst = w1_grp[:].rearrange("p t m j -> p m j t")
+        w1_src = w1_raw[:].rearrange("p j (m t) -> p m t j", t=PACK)
+        w1_dst = w1_grp[:].rearrange("p t m j -> p m t j")
         nc.vector.tensor_copy(w1_dst[:, 0:W1_SPLIT], w1_src[:, 0:W1_SPLIT])
         nc.scalar.copy(w1_dst[:, W1_SPLIT:P], w1_src[:, W1_SPLIT:P])
 
         xs_g = keep.tile([P, S], U8, name="xs_g", align_bytes=64)
         nc.vector.tensor_copy(xs_g[:], xs[:].indirect(offs_l[:]))
+
         w1_q = keep.tile([P, H], U32, name="w1_q", align_bytes=64)
         w1_s = keep.tile([P, H], U8, name="w1_s", align_bytes=64)
         nc.vector.quantize_mx(w1_q[:].bitcast(FP8X4), w1_s[:], w1_grp[:].rearrange("p t m j -> p (t m j)"))
 
-        xw_g = [keep.tile([P, hi - lo], U32, name=f"xw_g{lo}", align_bytes=64) for lo, hi in HALVES]
-        for u, (lo, hi) in enumerate(HALVES):
-            nc.vector.tensor_copy(xw_g[u][:], xw[:].indirect(entries(offs_l, lo, hi)))
+        xw_g = keep.tile([P, S], U32, name="xw_g", align_bytes=64)
+        for lo, hi in HALVES:
+            nc.vector.tensor_copy(xw_g[:, lo:hi], xw[:].indirect(entries(offs_l, lo, hi)))
+
+        def product(bank, w_q, w_s, t, v_q, v_s, lo, hi):
+            cols = slice(t * P, (t + 1) * P)
+            nc.tensor.matmul_mx(
+                out=bank[:, lo:hi],
+                lhsT=w_q[:, cols].bitcast(FP8X4),
+                lhsT_scale=w_s[:, cols],
+                rhs=v_q[:, lo:hi].bitcast(FP8X4),
+                rhs_scale=v_s[:, lo:hi],
+                start=True,
+                stop=True,
+            )
 
         y_ps = [psum.tile([P, S], F32, name=f"y_ps{t}") for t in range(PACK)]
-        y_w = rows("y_w", S)
-        for u, (lo, hi) in enumerate(HALVES):
-            for t in range(PACK):
-                cols = slice(t * P, (t + 1) * P)
-                nc.tensor.matmul_mx(
-                    out=y_ps[t][:, lo:hi],
-                    lhsT=w1_q[:, cols].bitcast(FP8X4),
-                    lhsT_scale=w1_s[:, cols],
-                    rhs=xw_g[u][:].bitcast(FP8X4),
-                    rhs_scale=xs_g[:, lo:hi],
-                    start=True,
-                    stop=True,
-                )
-                nc.scalar.copy(y_w[t][:, lo:hi], y_ps[t][:, lo:hi])
-
-        first = rows("first", S)
-        for lo, hi in HALVES:
-            for t in range(PACK):
-                nc.vector.tensor_tensor(first[t][:, lo:hi], tab_w[t][:].indirect(entries(n1_l, lo, hi)), y_w[t][:, lo:hi], ALU.add)
+        hneg_w = rows("hneg_w", 2 * S)
+        st_w = rows("st_w", 2 * S)
+        y_sb = [y_w[t][:, :S] for t in range(PACK)]
+        larger = [hneg_w[t][:, S:] for t in range(PACK)]
+        first = [y_w[t % 2][:, S:] for t in range(PACK)]
+        second = [y_w[u][:, S:] for u in (2, 3, 3, 2)]
+        h_sb = [st_w[t][:, S:] for t in range(PACK)]
+        for t in range(PACK):
+            for lo, hi in HALVES:
+                product(y_ps[t], w1_q, w1_s, t, xw_g, xs_g, lo, hi)
+                if t == 0:
+                    nc.scalar.copy(y_sb[t][:, lo:hi], y_ps[t][:, lo:hi])
+            if t > 0:
+                nc.scalar.copy(y_sb[t], y_ps[t][:])
 
         w2_grp = keep.tile([P, PACK, P, PACK], BF16, name="w2_grp", align_bytes=64)
         for u in range(2):
             nc.scalar.copy(
-                w2_grp[:, :, u * 64 : (u + 1) * 64, :].rearrange("p t m j -> p m j t"),
-                w2_raw[u][:].rearrange("p j (m t) -> p m j t", t=PACK),
+                w2_grp[:, :, u * 64 : (u + 1) * 64, :].rearrange("p t m j -> p m t j"),
+                w2_raw[u][:].rearrange("p j (m t) -> p m t j", t=PACK),
             )
+
+        z16 = keep.tile([P, S, PACK], BF16, name="z16", align_bytes=64)
+
+        def add_kind(t, lo, hi):
+            nc.vector.tensor_tensor(first[t][:, lo:hi], tab_w[t][:].indirect(entries(n1_l, lo, hi)), y_sb[t][:, lo:hi], ALU.add)
+
+        def fetch_y(t, lo, hi):
+            nc.vector.tensor_copy(second[t][:, lo:hi], y_w[t][:].indirect(entries(n2_l, lo, hi)))
+
+        def make_z(t, lo, hi):
+            nc.vector.tensor_tensor(larger[t][:, lo:hi], first[t][:, lo:hi], second[t][:, lo:hi], ALU.max)
+            nc.scalar.activation(z16[:, lo:hi, t], larger[t][:, lo:hi], COPY, scale=gain[:, t : t + 1])
+
+        for lo, hi in HALVES:
+            add_kind(0, lo, hi)
+        add_kind(1, 0, S)
+        fetch_y(0, 0, S)
+        fetch_y(1, 0, S)
+        make_z(0, 0, S)
+        make_z(1, 0, S)
+        add_kind(2, 0, S)
+        fetch_y(2, 0, S)
+        add_kind(3, 0, S)
+        make_z(2, 0, S)
+        fetch_y(3, 0, 256)
         w2_q = keep.tile([P, N], U32, name="w2_q", align_bytes=64)
         w2_s = keep.tile([P, N], U8, name="w2_s", align_bytes=64)
         nc.vector.quantize_mx(w2_q[:].bitcast(FP8X4), w2_s[:], w2_grp[:].rearrange("p t m j -> p (t m j)"))
+        make_z(3, 0, 256)
+        fetch_y(3, 256, S)
+        for lo, hi in Z_CHUNKS[1:]:
+            make_z(3, lo, hi)
 
-        second = rows("second", S)
-        larger = rows("larger", S)
+        z_q = keep.tile([P, S], U32, name="z_q", align_bytes=64)
+        z_s = keep.tile([P, S], U8, name="z_s", align_bytes=64)
         h_ps = [psum.tile([P, S], F32, name=f"h_ps{t}") for t in range(PACK)]
-        hneg_w = rows("hneg_w", S)
-        h_sb = rows("h_sb", S)
         for lo, hi in Z_CHUNKS:
-            z16 = keep.tile([P, hi - lo, PACK], BF16, name=f"z16_{lo}", align_bytes=64)
-            for t in range(PACK):
-                nc.vector.tensor_copy(second[t][:, lo:hi], y_w[t][:].indirect(entries(n2_l, lo, hi)))
-                nc.vector.tensor_tensor(larger[t][:, lo:hi], first[t][:, lo:hi], second[t][:, lo:hi], ALU.max)
-                nc.scalar.activation(z16[:, :, t], larger[t][:, lo:hi], COPY, scale=gain[:, t : t + 1])
-            z_q = keep.tile([P, hi - lo], U32, name=f"z_q{lo}", align_bytes=64)
-            z_s = keep.tile([P, hi - lo], U8, name=f"z_s{lo}", align_bytes=64)
-            nc.vector.quantize_mx(z_q[:].bitcast(FP8X4), z_s[:], z16[:].rearrange("p n t -> p (n t)"))
-            for t in range(PACK):
-                cols = slice(t * P, (t + 1) * P)
-                nc.tensor.matmul_mx(
-                    out=h_ps[t][:, lo:hi],
-                    lhsT=w2_q[:, cols].bitcast(FP8X4),
-                    lhsT_scale=w2_s[:, cols],
-                    rhs=z_q[:].bitcast(FP8X4),
-                    rhs_scale=z_s[:],
-                    start=True,
-                    stop=True,
-                )
+            nc.vector.quantize_mx(z_q[:, lo:hi].bitcast(FP8X4), z_s[:, lo:hi], z16[:, lo:hi, :].rearrange("p n t -> p (n t)"))
+            product(h_ps[0], w2_q, w2_s, 0, z_q, z_s, lo, hi)
             nc.scalar.activation(hneg_w[0][:, lo:hi], h_ps[0][:, lo:hi], COPY, scale=-1.0)
-            nc.scalar.copy(h_sb[0][:, lo:hi], h_ps[0][:, lo:hi])
+            if lo == 0:
+                nc.scalar.copy(h_sb[0][:, lo:hi], h_ps[0][:, lo:hi])
+                for t in range(1, PACK):
+                    product(h_ps[t], w2_q, w2_s, t, z_q, z_s, lo, hi)
+        nc.scalar.copy(h_sb[0][:, 256:S], h_ps[0][:, 256:S])
         for t in range(1, PACK):
-            nc.scalar.activation(hneg_w[t][:], h_ps[t][:], COPY, scale=-1.0)
-            nc.scalar.copy(h_sb[t][:], h_ps[t][:])
+            product(h_ps[t], w2_q, w2_s, t, z_q, z_s, 256, S)
+            nc.scalar.activation(hneg_w[t][:, :S], h_ps[t][:], COPY, scale=-1.0)
+            nc.scalar.copy(h_sb[t], h_ps[t][:])
 
-        st_w = rows("st_w", S)
         other = rows("other", S)
         res = rows("res", S)
         out_rows = out.rearrange("(p t) c -> p t c", t=PACK)
 
-        def step(t):
-            for lo, hi in HALVES:
-                nc.vector.tensor_tensor(st_w[t][:, lo:hi], hneg_w[t][:].indirect(entries(n3_l, lo, hi)), h_sb[t][:, lo:hi], ALU.add)
+        def step(t, lo, hi):
+            nc.vector.tensor_tensor(st_w[t][:, lo:hi], hneg_w[t][:].indirect(entries(n3_l, lo, hi)), h_sb[t][:, lo:hi], ALU.add)
 
-        def finish(t):
-            for lo, hi in HALVES:
-                nc.vector.tensor_copy(other[t][:, lo:hi], st_w[t][:].indirect(entries(n4_l, lo, hi)))
-            for lo, hi in HALVES:
-                nc.vector.tensor_tensor(res[t][:, lo:hi], st_w[t][:, lo:hi], other[t][:, lo:hi], ALU.max)
-                nc.sync.dma_start(out_rows[:, t, lo:hi], res[t][:, lo:hi])
+        def fetch_st(t, lo, hi):
+            nc.vector.tensor_copy(other[t][:, lo:hi], st_w[t][:].indirect(entries(n4_l, lo, hi)))
 
-        step(0)
-        for t in range(1, PACK):
-            step(t)
-            finish(t - 1)
-        finish(PACK - 1)
+        def finish(t, lo, hi):
+            nc.vector.tensor_tensor(res[t][:, lo:hi], st_w[t][:, lo:hi], other[t][:, lo:hi], ALU.max)
+            nc.sync.dma_start(out_rows[:, t, lo:hi], res[t][:, lo:hi])
+
+        for lo, hi in HALVES:
+            step(0, lo, hi)
+        step(1, 0, S)
+        fetch_st(0, 0, S)
+        step(2, 0, S)
+        finish(0, 0, S)
+        fetch_st(1, 0, S)
+        step(3, 0, S)
+        finish(1, 0, S)
+        fetch_st(2, 0, S)
+        fetch_st(3, 0, 256)
+        finish(2, 0, S)
+        fetch_st(3, 256, S)
+        for lo, hi in HALVES:
+            finish(3, lo, hi)

@@ -1,6 +1,7 @@
 from contextlib import ExitStack
 
 import concourse.mybir as mybir
+from concourse.masks import make_identity
 
 K, T, S, N, H, J = 512, 2048, 512, 512, 512, 512
 FLOPS = 2 * K * H * S + 2 * H * N * S
@@ -14,11 +15,12 @@ U8 = mybir.dt.uint8
 FP8X4 = mybir.dt.float8_e4m3fn_x4
 ALU = mybir.AluOpType
 COPY = mybir.ActivationFunctionType.Copy
+RELU = mybir.ActivationFunctionType.Relu
 
 P = 128
 PACK = 4
 STRIPE = 16
-W1_SPLIT = 80
+W1_SPLIT = 32
 HALVES = [(0, 256), (256, 512)]
 Z_CHUNKS = [(0, 256), (256, 384), (384, 512)]
 
@@ -44,6 +46,11 @@ def tile_picked_laykindhopmx_none_p_kernel(
 
         xs = keep.tile([P, T], U8, name="xs", align_bytes=64)
         nc.vector.memset(xs[:].bitcast(I32), 0)
+        n1_l = load_list("n1_l", n1)
+        tab_rows = tab.rearrange("(p t) c -> p t c", t=PACK)
+        tab_w = rows("tab_w", J)
+        for t in range(PACK - 1):
+            nc.sync.dma_start(tab_w[t][:], tab_rows[:, t, :])
         w1_raw = keep.tile([P, PACK, H], F32, name="w1_raw")
         nc.sync.dma_start(w1_raw[:], w1.rearrange("(p j) c -> p j c", j=PACK))
         for q in range(4):
@@ -51,29 +58,30 @@ def tile_picked_laykindhopmx_none_p_kernel(
         offs_l = load_list("offs_l", offs)
         xw = keep.tile([P, T], U32, name="xw", align_bytes=64)
         nc.sync.dma_start(xw[:].bitcast(I32), x_words[0].rearrange("p n r -> p (n r)").bitcast(I32))
-        n1_l = load_list("n1_l", n1)
-        tab_rows = tab.rearrange("(p t) c -> p t c", t=PACK)
-        tab_w = rows("tab_w", 2 * J)
-        y_w = rows("y_w", 2 * S)
-        for t in range(PACK):
-            nc.vector.memset(tab_w[t][:, J:], 0.0)
+        nc.sync.dma_start(tab_w[PACK - 1][:], tab_rows[:, PACK - 1, :])
+        n2_l = load_list("n2_l", n2)
         w2_rows = w2.rearrange("(p j) c -> p j c", j=PACK)
         w2_raw = [keep.tile([P, PACK, N // 2], F32, name=f"w2_raw{u}") for u in range(2)]
-        nc.sync.dma_start(tab_w[0][:, :J], tab_rows[:, 0, :])
-        nc.sync.dma_start(tab_w[1][:, :J], tab_rows[:, 1, :])
-        n2_l = load_list("n2_l", n2)
-        nc.sync.dma_start(w2_raw[0][:], w2_rows[:, :, 0 : N // 2])
-        nc.sync.dma_start(tab_w[2][:, :J], tab_rows[:, 2, :])
+        for u in range(2):
+            nc.sync.dma_start(w2_raw[u][:], w2_rows[:, :, u * N // 2 : (u + 1) * N // 2])
         gain = keep.tile([P, PACK], F32, name="gain")
         nc.sync.dma_start(gain[:], gn.rearrange("(p t) o -> p (t o)", t=PACK))
-        nc.sync.dma_start(w2_raw[1][:], w2_rows[:, :, N // 2 : N])
-        nc.sync.dma_start(tab_w[3][:, :J], tab_rows[:, 3, :])
         n3_l = load_list("n3_l", n3)
         n4_l = load_list("n4_l", n4)
 
+        y_w = rows("y_w", 2 * S)
+        kind = [y_w[t][:, S:] for t in range(PACK)]
+
+        def fetch_kind(t):
+            for lo, hi in HALVES:
+                nc.vector.tensor_copy(kind[t][:, lo:hi], tab_w[t][:].indirect(entries(n1_l, lo, hi)))
+
+        for t in range(PACK - 1):
+            fetch_kind(t)
+
         w1_grp = keep.tile([P, PACK, P, PACK], BF16, name="w1_grp", align_bytes=64)
-        w1_src = w1_raw[:].rearrange("p j (m t) -> p m t j", t=PACK)
-        w1_dst = w1_grp[:].rearrange("p t m j -> p m t j")
+        w1_src = w1_raw[:].rearrange("p j (m t) -> p m j t", t=PACK)
+        w1_dst = w1_grp[:].rearrange("p t m j -> p m j t")
         nc.vector.tensor_copy(w1_dst[:, 0:W1_SPLIT], w1_src[:, 0:W1_SPLIT])
         nc.scalar.copy(w1_dst[:, W1_SPLIT:P], w1_src[:, W1_SPLIT:P])
 
@@ -100,33 +108,32 @@ def tile_picked_laykindhopmx_none_p_kernel(
                 stop=True,
             )
 
-        y_ps = [psum.tile([P, S], F32, name=f"y_ps{t}") for t in range(PACK)]
+        bank = [psum.tile([P, S], F32, name=f"bank{b}") for b in range(8)]
         hneg_w = rows("hneg_w", 2 * S)
         st_w = rows("st_w", 2 * S)
         y_sb = [y_w[t][:, :S] for t in range(PACK)]
         larger = [hneg_w[t][:, S:] for t in range(PACK)]
-        first = [y_w[t % 2][:, S:] for t in range(PACK)]
-        second = [y_w[u][:, S:] for u in (2, 3, 3, 2)]
+        first = rows("first", S)
+        second = rows("second", S)
         h_sb = [st_w[t][:, S:] for t in range(PACK)]
-        for t in range(PACK):
-            for lo, hi in HALVES:
-                product(y_ps[t], w1_q, w1_s, t, xw_g, xs_g, lo, hi)
-                if t == 0:
-                    nc.scalar.copy(y_sb[t][:, lo:hi], y_ps[t][:, lo:hi])
-            if t > 0:
-                nc.scalar.copy(y_sb[t], y_ps[t][:])
+        for u, (lo, hi) in enumerate(HALVES):
+            product(bank[u], w1_q, w1_s, 0, xw_g, xs_g, lo, hi)
+            nc.scalar.copy(y_sb[0][:, lo:hi], bank[u][:, lo:hi])
+        for t in range(1, PACK):
+            product(bank[t + 1], w1_q, w1_s, t, xw_g, xs_g, 0, S)
+            nc.scalar.copy(y_sb[t], bank[t + 1][:])
 
         w2_grp = keep.tile([P, PACK, P, PACK], BF16, name="w2_grp", align_bytes=64)
         for u in range(2):
             nc.scalar.copy(
-                w2_grp[:, :, u * 64 : (u + 1) * 64, :].rearrange("p t m j -> p m t j"),
-                w2_raw[u][:].rearrange("p j (m t) -> p m t j", t=PACK),
+                w2_grp[:, :, u * 64 : (u + 1) * 64, :].rearrange("p t m j -> p m j t"),
+                w2_raw[u][:].rearrange("p j (m t) -> p m j t", t=PACK),
             )
 
         z16 = keep.tile([P, S, PACK], BF16, name="z16", align_bytes=64)
 
-        def add_kind(t, lo, hi):
-            nc.vector.tensor_tensor(first[t][:, lo:hi], tab_w[t][:].indirect(entries(n1_l, lo, hi)), y_sb[t][:, lo:hi], ALU.add)
+        def add_kind(t):
+            nc.vector.tensor_tensor(first[t][:], kind[t], y_sb[t], ALU.add)
 
         def fetch_y(t, lo, hi):
             nc.vector.tensor_copy(second[t][:, lo:hi], y_w[t][:].indirect(entries(n2_l, lo, hi)))
@@ -135,45 +142,50 @@ def tile_picked_laykindhopmx_none_p_kernel(
             nc.vector.tensor_tensor(larger[t][:, lo:hi], first[t][:, lo:hi], second[t][:, lo:hi], ALU.max)
             nc.scalar.activation(z16[:, lo:hi, t], larger[t][:, lo:hi], COPY, scale=gain[:, t : t + 1])
 
-        for lo, hi in HALVES:
-            add_kind(0, lo, hi)
-        add_kind(1, 0, S)
-        fetch_y(0, 0, S)
-        fetch_y(1, 0, S)
-        make_z(0, 0, S)
-        make_z(1, 0, S)
-        add_kind(2, 0, S)
-        fetch_y(2, 0, S)
-        add_kind(3, 0, S)
-        make_z(2, 0, S)
-        fetch_y(3, 0, 256)
         w2_q = keep.tile([P, N], U32, name="w2_q", align_bytes=64)
         w2_s = keep.tile([P, N], U8, name="w2_s", align_bytes=64)
-        nc.vector.quantize_mx(w2_q[:].bitcast(FP8X4), w2_s[:], w2_grp[:].rearrange("p t m j -> p (t m j)"))
+
+        def quantise_w2(u):
+            cols = slice(u * N // 2, (u + 1) * N // 2)
+            nc.vector.quantize_mx(
+                w2_q[:, cols].bitcast(FP8X4), w2_s[:, cols], w2_grp[:, 2 * u : 2 * u + 2].rearrange("p t m j -> p (t m j)")
+            )
+
+        fetch_kind(PACK - 1)
+        add_kind(0)
+        for t in range(PACK - 1):
+            fetch_y(t, 0, S)
+            add_kind(t + 1)
+            make_z(t, 0, S)
+        fetch_y(3, 0, 256)
+        quantise_w2(0)
         make_z(3, 0, 256)
         fetch_y(3, 256, S)
+        quantise_w2(1)
         for lo, hi in Z_CHUNKS[1:]:
             make_z(3, lo, hi)
 
         z_q = keep.tile([P, S], U32, name="z_q", align_bytes=64)
         z_s = keep.tile([P, S], U8, name="z_s", align_bytes=64)
-        h_ps = [psum.tile([P, S], F32, name=f"h_ps{t}") for t in range(PACK)]
-        for lo, hi in Z_CHUNKS:
+        for u, (lo, hi) in enumerate(Z_CHUNKS):
             nc.vector.quantize_mx(z_q[:, lo:hi].bitcast(FP8X4), z_s[:, lo:hi], z16[:, lo:hi, :].rearrange("p n t -> p (n t)"))
-            product(h_ps[0], w2_q, w2_s, 0, z_q, z_s, lo, hi)
-            nc.scalar.activation(hneg_w[0][:, lo:hi], h_ps[0][:, lo:hi], COPY, scale=-1.0)
-            if lo == 0:
-                nc.scalar.copy(h_sb[0][:, lo:hi], h_ps[0][:, lo:hi])
-                for t in range(1, PACK):
-                    product(h_ps[t], w2_q, w2_s, t, z_q, z_s, lo, hi)
-        nc.scalar.copy(h_sb[0][:, 256:S], h_ps[0][:, 256:S])
+            product(bank[5 + u], w2_q, w2_s, 0, z_q, z_s, lo, hi)
+            nc.scalar.activation(hneg_w[0][:, lo:hi], bank[5 + u][:, lo:hi], COPY, scale=-1.0)
+            if u == 0:
+                nc.scalar.copy(h_sb[0][:, lo:hi], bank[5][:, lo:hi])
+        for u, (lo, hi) in list(enumerate(Z_CHUNKS))[1:]:
+            nc.scalar.copy(h_sb[0][:, lo:hi], bank[5 + u][:, lo:hi])
         for t in range(1, PACK):
-            product(h_ps[t], w2_q, w2_s, t, z_q, z_s, 256, S)
-            nc.scalar.activation(hneg_w[t][:, :S], h_ps[t][:], COPY, scale=-1.0)
-            nc.scalar.copy(h_sb[t], h_ps[t][:])
+            product(bank[t - 1], w2_q, w2_s, t, z_q, z_s, 0, S)
+            nc.scalar.activation(hneg_w[t][:, :S], bank[t - 1][:], COPY, scale=-1.0)
+            nc.scalar.copy(h_sb[t], bank[t - 1][:])
 
+        ident = keep.tile([P, P], F32, name="ident")
+        make_identity(nc, ident[:])
         other = rows("other", S)
         res = rows("res", S)
+        st_turned = rows("st_turned", S)
+        excess = rows("excess", S)
         out_rows = out.rearrange("(p t) c -> p t c", t=PACK)
 
         def step(t, lo, hi):
@@ -186,15 +198,29 @@ def tile_picked_laykindhopmx_none_p_kernel(
             nc.vector.tensor_tensor(res[t][:, lo:hi], st_w[t][:, lo:hi], other[t][:, lo:hi], ALU.max)
             nc.sync.dma_start(out_rows[:, t, lo:hi], res[t][:, lo:hi])
 
+        def turn_sum(target, *terms):
+            for u in range(S // P):
+                cols = slice(u * P, (u + 1) * P)
+                for i, term in enumerate(terms):
+                    nc.tensor.matmul(target[:, cols], term[:, cols], ident[:], start=(i == 0), stop=(i == len(terms) - 1), is_transpose=True)
+
+        def finish_turned(t, b_st, b_diff, b_out):
+            turn_sum(b_st, st_w[t])
+            nc.scalar.copy(st_turned[t][:], b_st[:])
+            nc.vector.tensor_scalar(other[t][:], st_w[t][:].indirect(n4_l[:]), -1.0, 0.0, ALU.mult, ALU.add)
+            turn_sum(b_diff, st_w[t], other[t])
+            nc.scalar.activation(excess[t][:], b_diff[:], RELU, scale=-1.0)
+            turn_sum(b_out, st_turned[t], excess[t])
+            nc.scalar.copy(res[t][:], b_out[:])
+            nc.scalar.dma_start(out_rows[:, t, :], res[t][:])
+
         for lo, hi in HALVES:
             step(0, lo, hi)
         step(1, 0, S)
-        fetch_st(0, 0, S)
+        finish_turned(0, bank[3], bank[4], bank[5])
         step(2, 0, S)
-        finish(0, 0, S)
-        fetch_st(1, 0, S)
+        finish_turned(1, bank[6], bank[7], bank[3])
         step(3, 0, S)
-        finish(1, 0, S)
         fetch_st(2, 0, S)
         fetch_st(3, 0, 256)
         finish(2, 0, S)

@@ -19,10 +19,15 @@ RELU = mybir.ActivationFunctionType.Relu
 
 P = 128
 PACK = 4
+LAST = PACK - 1
 STRIPE = 16
-W1_SPLIT = 32
-HALVES = [(0, 256), (256, 512)]
-Z_CHUNKS = [(0, 256), (256, 384), (384, 512)]
+QUADRANT = 32
+RUN = 4
+BANKS = 8
+HALVES = [(0, S // 2), (S // 2, S)]
+W1_ON_VECTOR = 32
+Z_PIECES = [(1, S // 2, S), (0, 0, S // 4), (0, S // 4, S // 2)]
+LAST_STORES = [(0, S // 2), (S // 2, 3 * S // 4), (3 * S // 4, S)]
 
 
 def tile_picked_laykindhopmx_none_p_kernel(
@@ -41,189 +46,214 @@ def tile_picked_laykindhopmx_none_p_kernel(
         def entries(held, lo, hi):
             return held[:, lo // STRIPE : hi // STRIPE]
 
-        def rows(name, width, dtype=F32):
-            return [keep.tile([P, width], dtype, name=f"{name}{t}", align_bytes=64) for t in range(PACK)]
+        def planes(name, width, count=PACK):
+            return [keep.tile([P, width], F32, name=f"{name}{t}", align_bytes=64) for t in range(count)]
 
-        xs = keep.tile([P, T], U8, name="xs", align_bytes=64)
-        nc.vector.memset(xs[:].bitcast(I32), 0)
-        n1_l = load_list("n1_l", n1)
+        x_bytes = keep.tile([P, T], U8, name="x_bytes", align_bytes=64)
+        nc.vector.memset(x_bytes[:].bitcast(I32), 0)
+        n1_list = load_list("n1_list", n1)
         tab_rows = tab.rearrange("(p t) c -> p t c", t=PACK)
-        tab_w = rows("tab_w", J)
-        for t in range(PACK - 1):
-            nc.sync.dma_start(tab_w[t][:], tab_rows[:, t, :])
+        tab_win = planes("tab_win", J)
+        gain = keep.tile([P, PACK], F32, name="gain")
+        nc.sync.dma_start(tab_win[0][:], tab_rows[:, 0, :])
+        nc.sync.dma_start(gain[:], gn.rearrange("(p t) o -> p (t o)", t=PACK))
+        for t in range(1, LAST):
+            nc.sync.dma_start(tab_win[t][:], tab_rows[:, t, :])
         w1_raw = keep.tile([P, PACK, H], F32, name="w1_raw")
         nc.sync.dma_start(w1_raw[:], w1.rearrange("(p j) c -> p j c", j=PACK))
-        for q in range(4):
-            nc.sync.dma_start(xs[32 * q : 32 * q + 4, :].bitcast(I32), x_scales[0, 4 * q : 4 * q + 4, :].bitcast(I32))
-        offs_l = load_list("offs_l", offs)
-        xw = keep.tile([P, T], U32, name="xw", align_bytes=64)
-        nc.sync.dma_start(xw[:].bitcast(I32), x_words[0].rearrange("p n r -> p (n r)").bitcast(I32))
-        nc.sync.dma_start(tab_w[PACK - 1][:], tab_rows[:, PACK - 1, :])
-        n2_l = load_list("n2_l", n2)
+        for q in range(P // QUADRANT):
+            nc.sync.dma_start(
+                x_bytes[QUADRANT * q : QUADRANT * q + 4, :].bitcast(I32), x_scales[0, 4 * q : 4 * q + 4, :].bitcast(I32)
+            )
+        offs_list = load_list("offs_list", offs)
+        x_codes = keep.tile([P, T], U32, name="x_codes", align_bytes=64)
+        nc.sync.dma_start(x_codes[:].bitcast(I32), x_words[0].rearrange("p n r -> p (n r)").bitcast(I32))
+        nc.sync.dma_start(tab_win[LAST][:], tab_rows[:, LAST, :])
+        n2_list = load_list("n2_list", n2)
         w2_rows = w2.rearrange("(p j) c -> p j c", j=PACK)
-        w2_raw = [keep.tile([P, PACK, N // 2], F32, name=f"w2_raw{u}") for u in range(2)]
+        w2_raw = [keep.tile([P, 2, N], F32, name=f"w2_raw{u}") for u in range(2)]
         for u in range(2):
-            nc.sync.dma_start(w2_raw[u][:], w2_rows[:, :, u * N // 2 : (u + 1) * N // 2])
-        gain = keep.tile([P, PACK], F32, name="gain")
-        nc.sync.dma_start(gain[:], gn.rearrange("(p t) o -> p (t o)", t=PACK))
-        n3_l = load_list("n3_l", n3)
-        n4_l = load_list("n4_l", n4)
+            nc.sync.dma_start(w2_raw[u][:], w2_rows[:, 2 * u : 2 * u + 2, :])
+        n3_list = load_list("n3_list", n3)
+        n4_list = load_list("n4_list", n4)
 
-        y_w = rows("y_w", 2 * S)
-        kind = [y_w[t][:, S:] for t in range(PACK)]
+        y_win = planes("y_win", 2 * S)
+        y_sized = [y_win[t][:, :S] for t in range(PACK)]
+        kind_sized = [y_win[t][:, S:] for t in range(PACK)]
+        hneg_win = planes("hneg_win", 2 * S)
+        kind_raw = [hneg_win[t][:, S:] for t in range(LAST)]
 
-        def fetch_kind(t):
+        twice_positive = keep.tile([P, PACK], F32, name="twice_positive")
+        gain_sign = keep.tile([P, PACK], F32, name="gain_sign")
+        gain_size = keep.tile([P, PACK], F32, name="gain_size")
+        nc.gpsimd.tensor_scalar(twice_positive[:], gain[:], 0.0, 2.0, ALU.is_ge, ALU.mult)
+        nc.gpsimd.tensor_scalar(gain_sign[:], twice_positive[:], 1.0, -1.0, ALU.mult, ALU.add)
+        nc.gpsimd.tensor_tensor(gain_size[:], gain[:], gain_sign[:], ALU.mult)
+
+        for t in range(LAST):
             for lo, hi in HALVES:
-                nc.vector.tensor_copy(kind[t][:, lo:hi], tab_w[t][:].indirect(entries(n1_l, lo, hi)))
+                nc.vector.tensor_copy(kind_raw[t][:, lo:hi], tab_win[t][:].indirect(entries(n1_list, lo, hi)))
+            nc.scalar.activation(kind_sized[t], kind_raw[t], COPY, scale=gain_size[:, t : t + 1])
 
-        for t in range(PACK - 1):
-            fetch_kind(t)
+        w1_woven = keep.tile([P, PACK, P, PACK], BF16, name="w1_woven", align_bytes=64)
+        w1_from = w1_raw[:].rearrange("p j (m t) -> p m j t", t=PACK)
+        w1_to = w1_woven[:].rearrange("p t m j -> p m j t")
+        nc.vector.tensor_copy(w1_to[:, 0:W1_ON_VECTOR], w1_from[:, 0:W1_ON_VECTOR])
+        nc.scalar.copy(w1_to[:, W1_ON_VECTOR:P], w1_from[:, W1_ON_VECTOR:P])
 
-        w1_grp = keep.tile([P, PACK, P, PACK], BF16, name="w1_grp", align_bytes=64)
-        w1_src = w1_raw[:].rearrange("p j (m t) -> p m j t", t=PACK)
-        w1_dst = w1_grp[:].rearrange("p t m j -> p m j t")
-        nc.vector.tensor_copy(w1_dst[:, 0:W1_SPLIT], w1_src[:, 0:W1_SPLIT])
-        nc.scalar.copy(w1_dst[:, W1_SPLIT:P], w1_src[:, W1_SPLIT:P])
+        picked_bytes = keep.tile([P, S], U8, name="picked_bytes", align_bytes=64)
+        nc.vector.tensor_copy(picked_bytes[:], x_bytes[:].indirect(offs_list[:]))
 
-        xs_g = keep.tile([P, S], U8, name="xs_g", align_bytes=64)
-        nc.vector.tensor_copy(xs_g[:], xs[:].indirect(offs_l[:]))
+        w1_codes = keep.tile([P, H], U32, name="w1_codes", align_bytes=64)
+        w1_bytes = keep.tile([P, H], U8, name="w1_bytes", align_bytes=64)
+        nc.vector.quantize_mx(w1_codes[:].bitcast(FP8X4), w1_bytes[:], w1_woven[:].rearrange("p t m j -> p (t m j)"))
 
-        w1_q = keep.tile([P, H], U32, name="w1_q", align_bytes=64)
-        w1_s = keep.tile([P, H], U8, name="w1_s", align_bytes=64)
-        nc.vector.quantize_mx(w1_q[:].bitcast(FP8X4), w1_s[:], w1_grp[:].rearrange("p t m j -> p (t m j)"))
-
-        xw_g = keep.tile([P, S], U32, name="xw_g", align_bytes=64)
+        picked_codes = keep.tile([P, S], U32, name="picked_codes", align_bytes=64)
         for lo, hi in HALVES:
-            nc.vector.tensor_copy(xw_g[:, lo:hi], xw[:].indirect(entries(offs_l, lo, hi)))
+            nc.vector.tensor_copy(picked_codes[:, lo:hi], x_codes[:].indirect(entries(offs_list, lo, hi)))
 
-        def product(bank, w_q, w_s, t, v_q, v_s, lo, hi):
-            cols = slice(t * P, (t + 1) * P)
+        tab_last_sized = keep.tile([P, J], F32, name="tab_last_sized", align_bytes=64)
+        nc.vector.memset(hneg_win[LAST][:, S:], 0.0)
+        nc.scalar.activation(tab_last_sized[:], tab_win[LAST][:], COPY, scale=gain_size[:, LAST : LAST + 1])
+        for lo, hi in HALVES:
+            nc.vector.tensor_copy(kind_sized[LAST][:, lo:hi], tab_last_sized[:].indirect(entries(n1_list, lo, hi)))
+
+        def product(target, w_codes, w_bytes, block, v_codes, v_bytes, lo, hi):
+            cols = slice(block * P, (block + 1) * P)
             nc.tensor.matmul_mx(
-                out=bank[:, lo:hi],
-                lhsT=w_q[:, cols].bitcast(FP8X4),
-                lhsT_scale=w_s[:, cols],
-                rhs=v_q[:, lo:hi].bitcast(FP8X4),
-                rhs_scale=v_s[:, lo:hi],
+                out=target[:, lo:hi],
+                lhsT=w_codes[:, cols].bitcast(FP8X4),
+                lhsT_scale=w_bytes[:, cols],
+                rhs=v_codes[:, lo:hi].bitcast(FP8X4),
+                rhs_scale=v_bytes[:, lo:hi],
                 start=True,
                 stop=True,
             )
 
-        bank = [psum.tile([P, S], F32, name=f"bank{b}") for b in range(8)]
-        hneg_w = rows("hneg_w", 2 * S)
-        st_w = rows("st_w", 2 * S)
-        y_sb = [y_w[t][:, :S] for t in range(PACK)]
-        larger = [hneg_w[t][:, S:] for t in range(PACK)]
-        first = rows("first", S)
-        second = rows("second", S)
-        h_sb = [st_w[t][:, S:] for t in range(PACK)]
+        bank = [psum.tile([P, S], F32, name=f"bank{b}") for b in range(BANKS)]
+        st_win = planes("st_win", 2 * S)
+        h_plain = [st_win[t][:, S:] for t in range(PACK)]
+        with_kind = keep.tile([P, PACK, S], BF16, name="with_kind", align_bytes=64)
+        y_fetched = keep.tile([P, PACK, S], BF16, name="y_fetched", align_bytes=64)
         for u, (lo, hi) in enumerate(HALVES):
-            product(bank[u], w1_q, w1_s, 0, xw_g, xs_g, lo, hi)
-            nc.scalar.copy(y_sb[0][:, lo:hi], bank[u][:, lo:hi])
+            product(bank[u], w1_codes, w1_bytes, 0, picked_codes, picked_bytes, lo, hi)
+            nc.scalar.activation(y_sized[0][:, lo:hi], bank[u][:, lo:hi], COPY, scale=gain_size[:, 0:1])
         for t in range(1, PACK):
-            product(bank[t + 1], w1_q, w1_s, t, xw_g, xs_g, 0, S)
-            nc.scalar.copy(y_sb[t], bank[t + 1][:])
+            product(bank[t + 1], w1_codes, w1_bytes, t, picked_codes, picked_bytes, 0, S)
+            nc.scalar.activation(y_sized[t], bank[t + 1][:], COPY, scale=gain_size[:, t : t + 1])
 
-        w2_grp = keep.tile([P, PACK, P, PACK], BF16, name="w2_grp", align_bytes=64)
-        for u in range(2):
-            nc.scalar.copy(
-                w2_grp[:, :, u * 64 : (u + 1) * 64, :].rearrange("p t m j -> p m j t"),
-                w2_raw[u][:].rearrange("p j (m t) -> p m j t", t=PACK),
+        w2_signed = keep.tile([P, PACK, N], BF16, name="w2_signed", tag="scratch16", align_bytes=64)
+        for j in range(PACK):
+            nc.scalar.activation(w2_signed[:, j, :], w2_raw[j // 2][:, j % 2, :], COPY, scale=gain_sign[:, j : j + 1])
+        w2_woven = keep.tile([P, PACK, P, PACK], BF16, name="w2_woven", align_bytes=64)
+        nc.scalar.copy(
+            w2_woven[:].rearrange("p t m j -> p m j t"),
+            w2_signed[:].rearrange("p j (m t) -> p m j t", t=PACK),
+        )
+
+        for t in range(PACK):
+            for lo, hi in HALVES if t == 0 else [(0, S)]:
+                nc.gpsimd.tensor_tensor(with_kind[:, t, lo:hi], kind_sized[t][:, lo:hi], y_sized[t][:, lo:hi], ALU.add)
+            nc.vector.tensor_copy(y_fetched[:, t, :], y_win[t][:].indirect(n2_list[:]))
+
+        larger = keep.tile([P, PACK, S], BF16, name="larger", tag=f"y_win{LAST}", align_bytes=64)
+        z_woven = [
+            keep.tile([P, S // 2, PACK], BF16, name="z_woven0", tag="scratch16", align_bytes=64),
+            keep.tile([P, S // 2, PACK], BF16, name="z_woven1", align_bytes=64),
+        ]
+        for lo, hi in HALVES:
+            nc.vector.tensor_tensor(larger[:, :, lo:hi], with_kind[:, :, lo:hi], y_fetched[:, :, lo:hi], ALU.max)
+
+        def z_piece(u, lo, hi):
+            return z_woven[u][:, lo - HALVES[u][0] : hi - HALVES[u][0], :]
+
+        def weave_z(copy, u, lo, hi):
+            copy(
+                z_piece(u, lo, hi).rearrange("p (c i) t -> p c t i", i=RUN),
+                larger[:, :, lo:hi].rearrange("p t (c i) -> p c t i", i=RUN),
             )
 
-        z16 = keep.tile([P, S, PACK], BF16, name="z16", align_bytes=64)
+        for piece in Z_PIECES[1:]:
+            weave_z(nc.scalar.copy, *piece)
+        weave_z(nc.vector.tensor_copy, *Z_PIECES[0])
 
-        def add_kind(t):
-            nc.vector.tensor_tensor(first[t][:], kind[t], y_sb[t], ALU.add)
+        def quantise_w2(u, **placed):
+            codes = keep.tile([P, N // 2], U32, name=f"w2_codes{u}", align_bytes=64, **placed)
+            scale_bytes = keep.tile([P, N // 2], U8, name=f"w2_bytes{u}", align_bytes=64)
+            source = w2_woven[:, 2 * u : 2 * u + 2].rearrange("p t m j -> p (t m j)")
+            nc.vector.quantize_mx(codes[:].bitcast(FP8X4), scale_bytes[:], source)
+            return codes, scale_bytes
 
-        def fetch_y(t, lo, hi):
-            nc.vector.tensor_copy(second[t][:, lo:hi], y_w[t][:].indirect(entries(n2_l, lo, hi)))
+        w2_low = quantise_w2(0)
 
-        def make_z(t, lo, hi):
-            nc.vector.tensor_tensor(larger[t][:, lo:hi], first[t][:, lo:hi], second[t][:, lo:hi], ALU.max)
-            nc.scalar.activation(z16[:, lo:hi, t], larger[t][:, lo:hi], COPY, scale=gain[:, t : t + 1])
-
-        w2_q = keep.tile([P, N], U32, name="w2_q", align_bytes=64)
-        w2_s = keep.tile([P, N], U8, name="w2_s", align_bytes=64)
-
-        def quantise_w2(u):
-            cols = slice(u * N // 2, (u + 1) * N // 2)
+        z_codes = keep.tile([P, S], U32, name="z_codes", align_bytes=64)
+        z_bytes = keep.tile([P, S], U8, name="z_bytes", align_bytes=64)
+        piece_banks = bank[BANKS - len(Z_PIECES) :]
+        for target, (u, lo, hi) in zip(piece_banks, Z_PIECES):
             nc.vector.quantize_mx(
-                w2_q[:, cols].bitcast(FP8X4), w2_s[:, cols], w2_grp[:, 2 * u : 2 * u + 2].rearrange("p t m j -> p (t m j)")
+                z_codes[:, lo:hi].bitcast(FP8X4), z_bytes[:, lo:hi], z_piece(u, lo, hi).rearrange("p n t -> p (n t)")
             )
-
-        fetch_kind(PACK - 1)
-        add_kind(0)
-        for t in range(PACK - 1):
-            fetch_y(t, 0, S)
-            add_kind(t + 1)
-            make_z(t, 0, S)
-        fetch_y(3, 0, 256)
-        quantise_w2(0)
-        make_z(3, 0, 256)
-        fetch_y(3, 256, S)
-        quantise_w2(1)
-        for lo, hi in Z_CHUNKS[1:]:
-            make_z(3, lo, hi)
-
-        z_q = keep.tile([P, S], U32, name="z_q", align_bytes=64)
-        z_s = keep.tile([P, S], U8, name="z_s", align_bytes=64)
-        for u, (lo, hi) in enumerate(Z_CHUNKS):
-            nc.vector.quantize_mx(z_q[:, lo:hi].bitcast(FP8X4), z_s[:, lo:hi], z16[:, lo:hi, :].rearrange("p n t -> p (n t)"))
-            product(bank[5 + u], w2_q, w2_s, 0, z_q, z_s, lo, hi)
-            nc.scalar.activation(hneg_w[0][:, lo:hi], bank[5 + u][:, lo:hi], COPY, scale=-1.0)
-            if u == 0:
-                nc.scalar.copy(h_sb[0][:, lo:hi], bank[5][:, lo:hi])
-        for u, (lo, hi) in list(enumerate(Z_CHUNKS))[1:]:
-            nc.scalar.copy(h_sb[0][:, lo:hi], bank[5 + u][:, lo:hi])
+            product(target, *w2_low, 0, z_codes, z_bytes, lo, hi)
+            nc.scalar.activation(hneg_win[0][:, lo:hi], target[:, lo:hi], COPY, scale=-1.0)
+            if u == 1:
+                nc.scalar.copy(h_plain[0][:, lo:hi], target[:, lo:hi])
+        for target, (u, lo, hi) in zip(piece_banks[1:], Z_PIECES[1:]):
+            nc.scalar.copy(h_plain[0][:, lo:hi], target[:, lo:hi])
+        w2_high = quantise_w2(1, tag="scratch16")
         for t in range(1, PACK):
-            product(bank[t - 1], w2_q, w2_s, t, z_q, z_s, 0, S)
-            nc.scalar.activation(hneg_w[t][:, :S], bank[t - 1][:], COPY, scale=-1.0)
-            nc.scalar.copy(h_sb[t], bank[t - 1][:])
+            product(bank[t - 1], *(w2_low if t < 2 else w2_high), t % 2, z_codes, z_bytes, 0, S)
+            nc.scalar.activation(hneg_win[t][:, :S], bank[t - 1][:], COPY, scale=-1.0)
+            nc.scalar.copy(h_plain[t], bank[t - 1][:])
 
-        ident = keep.tile([P, P], F32, name="ident")
-        make_identity(nc, ident[:])
-        other = rows("other", S)
-        res = rows("res", S)
-        st_turned = rows("st_turned", S)
-        excess = rows("excess", S)
+        identity = keep.tile([P, P], F32, name="identity")
+        make_identity(nc, identity[:])
+        st_fetched = planes("st_fetched", S)
+        result = planes("result", S)
+        st_turned = planes("st_turned", S, 2)
+        excess_turned = planes("excess_turned", S, 2)
         out_rows = out.rearrange("(p t) c -> p t c", t=PACK)
 
-        def step(t, lo, hi):
-            nc.vector.tensor_tensor(st_w[t][:, lo:hi], hneg_w[t][:].indirect(entries(n3_l, lo, hi)), h_sb[t][:, lo:hi], ALU.add)
+        def make_st(t, lo, hi):
+            nc.vector.tensor_tensor(
+                st_win[t][:, lo:hi], hneg_win[t][:].indirect(entries(n3_list, lo, hi)), h_plain[t][:, lo:hi], ALU.add
+            )
 
         def fetch_st(t, lo, hi):
-            nc.vector.tensor_copy(other[t][:, lo:hi], st_w[t][:].indirect(entries(n4_l, lo, hi)))
+            nc.vector.tensor_copy(st_fetched[t][:, lo:hi], st_win[t][:].indirect(entries(n4_list, lo, hi)))
 
-        def finish(t, lo, hi):
-            nc.vector.tensor_tensor(res[t][:, lo:hi], st_w[t][:, lo:hi], other[t][:, lo:hi], ALU.max)
-            nc.sync.dma_start(out_rows[:, t, lo:hi], res[t][:, lo:hi])
+        def finish_on_vector(t, lo, hi):
+            nc.vector.tensor_tensor(result[t][:, lo:hi], st_win[t][:, lo:hi], st_fetched[t][:, lo:hi], ALU.max)
+            nc.sync.dma_start(out_rows[:, t, lo:hi], result[t][:, lo:hi])
 
         def turn_sum(target, *terms):
-            for u in range(S // P):
-                cols = slice(u * P, (u + 1) * P)
+            for block in range(S // P):
+                cols = slice(block * P, (block + 1) * P)
                 for i, term in enumerate(terms):
-                    nc.tensor.matmul(target[:, cols], term[:, cols], ident[:], start=(i == 0), stop=(i == len(terms) - 1), is_transpose=True)
+                    nc.tensor.matmul(
+                        target[:, cols], term[:, cols], identity[:],
+                        start=(i == 0), stop=(i == len(terms) - 1), is_transpose=True,
+                    )
 
-        def finish_turned(t, b_st, b_diff, b_out):
-            turn_sum(b_st, st_w[t])
-            nc.scalar.copy(st_turned[t][:], b_st[:])
-            nc.vector.tensor_scalar(other[t][:], st_w[t][:].indirect(n4_l[:]), -1.0, 0.0, ALU.mult, ALU.add)
-            turn_sum(b_diff, st_w[t], other[t])
-            nc.scalar.activation(excess[t][:], b_diff[:], RELU, scale=-1.0)
-            turn_sum(b_out, st_turned[t], excess[t])
-            nc.scalar.copy(res[t][:], b_out[:])
-            nc.scalar.dma_start(out_rows[:, t, :], res[t][:])
+        def finish_by_relu(t, st_bank, diff_bank, out_bank):
+            turn_sum(st_bank, st_win[t])
+            nc.scalar.copy(st_turned[t][:], st_bank[:])
+            nc.vector.tensor_scalar(st_fetched[t][:], st_win[t][:].indirect(n4_list[:]), -1.0, 0.0, ALU.mult, ALU.add)
+            turn_sum(diff_bank, st_win[t], st_fetched[t])
+            nc.scalar.activation(excess_turned[t][:], diff_bank[:], RELU, scale=-1.0)
+            turn_sum(out_bank, st_turned[t], excess_turned[t])
+            nc.scalar.copy(result[t][:], out_bank[:])
+            nc.scalar.dma_start(out_rows[:, t, :], result[t][:])
 
-        for lo, hi in HALVES:
-            step(0, lo, hi)
-        step(1, 0, S)
-        finish_turned(0, bank[3], bank[4], bank[5])
-        step(2, 0, S)
-        finish_turned(1, bank[6], bank[7], bank[3])
-        step(3, 0, S)
+        for lo, hi in reversed(HALVES):
+            make_st(0, lo, hi)
+        make_st(1, 0, S)
+        finish_by_relu(0, bank[3], bank[4], bank[5])
+        make_st(2, 0, S)
+        finish_by_relu(1, bank[6], bank[7], bank[3])
+        make_st(LAST, 0, S)
         fetch_st(2, 0, S)
-        fetch_st(3, 0, 256)
-        finish(2, 0, S)
-        fetch_st(3, 256, S)
-        for lo, hi in HALVES:
-            finish(3, lo, hi)
+        fetch_st(LAST, *HALVES[0])
+        finish_on_vector(2, 0, S)
+        fetch_st(LAST, *HALVES[1])
+        for lo, hi in LAST_STORES:
+            finish_on_vector(LAST, lo, hi)

from contextlib import ExitStack

import concourse.mybir as mybir
from concourse.masks import make_identity

K, T, S, N, H, J = 512, 2048, 512, 512, 512, 512
FLOPS = 2 * K * H * S + 2 * H * N * S

F32 = mybir.dt.float32
BF16 = mybir.dt.bfloat16
I32 = mybir.dt.int32
U32 = mybir.dt.uint32
U16 = mybir.dt.uint16
U8 = mybir.dt.uint8
FP8X4 = mybir.dt.float8_e4m3fn_x4
ALU = mybir.AluOpType
COPY = mybir.ActivationFunctionType.Copy
RELU = mybir.ActivationFunctionType.Relu

P = 128
PACK = 4
LAST = PACK - 1
STRIPE = 16
QUADRANT = 32
RUN = 4
BANKS = 8
HALVES = [(0, S // 2), (S // 2, S)]
W1_ON_VECTOR = 32
Z_PIECES = [(1, S // 2, S), (0, 0, S // 4), (0, S // 4, S // 2)]
LAST_STORES = [(0, S // 2), (S // 2, 3 * S // 4), (3 * S // 4, S)]


def tile_picked_laykindhopmx_none_p_kernel(
    tc, x_words, x_scales, w1, tab, gn, w2, offs, n1, n2, n3, n4, out
):
    nc = tc.nc
    with ExitStack() as ctx:
        keep = ctx.enter_context(tc.tile_pool(name="keep", bufs=1))
        psum = ctx.enter_context(tc.psum_pool(name="psum", bufs=1))

        def load_list(name, dram):
            held = keep.tile([P, S // STRIPE], U16, name=name)
            nc.sync.dma_start(held[:], dram)
            return held

        def entries(held, lo, hi):
            return held[:, lo // STRIPE : hi // STRIPE]

        def planes(name, width, count=PACK):
            return [keep.tile([P, width], F32, name=f"{name}{t}", align_bytes=64) for t in range(count)]

        x_bytes = keep.tile([P, T], U8, name="x_bytes", align_bytes=64)
        nc.vector.memset(x_bytes[:].bitcast(I32), 0)
        n1_list = load_list("n1_list", n1)
        tab_rows = tab.rearrange("(p t) c -> p t c", t=PACK)
        tab_win = planes("tab_win", J)
        gain = keep.tile([P, PACK], F32, name="gain")
        nc.sync.dma_start(tab_win[0][:], tab_rows[:, 0, :])
        nc.sync.dma_start(gain[:], gn.rearrange("(p t) o -> p (t o)", t=PACK))
        for t in range(1, LAST):
            nc.sync.dma_start(tab_win[t][:], tab_rows[:, t, :])
        w1_raw = keep.tile([P, PACK, H], F32, name="w1_raw")
        nc.sync.dma_start(w1_raw[:], w1.rearrange("(p j) c -> p j c", j=PACK))
        for q in range(P // QUADRANT):
            nc.sync.dma_start(
                x_bytes[QUADRANT * q : QUADRANT * q + 4, :].bitcast(I32), x_scales[0, 4 * q : 4 * q + 4, :].bitcast(I32)
            )
        offs_list = load_list("offs_list", offs)
        x_codes = keep.tile([P, T], U32, name="x_codes", align_bytes=64)
        nc.sync.dma_start(x_codes[:].bitcast(I32), x_words[0].rearrange("p n r -> p (n r)").bitcast(I32))
        nc.sync.dma_start(tab_win[LAST][:], tab_rows[:, LAST, :])
        n2_list = load_list("n2_list", n2)
        w2_rows = w2.rearrange("(p j) c -> p j c", j=PACK)
        w2_raw = [keep.tile([P, 2, N], F32, name=f"w2_raw{u}") for u in range(2)]
        for u in range(2):
            nc.sync.dma_start(w2_raw[u][:], w2_rows[:, 2 * u : 2 * u + 2, :])
        n3_list = load_list("n3_list", n3)
        n4_list = load_list("n4_list", n4)

        y_win = planes("y_win", 2 * S)
        y_sized = [y_win[t][:, :S] for t in range(PACK)]
        kind_sized = [y_win[t][:, S:] for t in range(PACK)]
        hneg_win = planes("hneg_win", 2 * S)
        kind_raw = [hneg_win[t][:, S:] for t in range(LAST)]

        twice_positive = keep.tile([P, PACK], F32, name="twice_positive")
        gain_sign = keep.tile([P, PACK], F32, name="gain_sign")
        gain_size = keep.tile([P, PACK], F32, name="gain_size")
        nc.gpsimd.tensor_scalar(twice_positive[:], gain[:], 0.0, 2.0, ALU.is_ge, ALU.mult)
        nc.gpsimd.tensor_scalar(gain_sign[:], twice_positive[:], 1.0, -1.0, ALU.mult, ALU.add)
        nc.gpsimd.tensor_tensor(gain_size[:], gain[:], gain_sign[:], ALU.mult)

        for t in range(LAST):
            for lo, hi in HALVES:
                nc.vector.tensor_copy(kind_raw[t][:, lo:hi], tab_win[t][:].indirect(entries(n1_list, lo, hi)))
            nc.scalar.activation(kind_sized[t], kind_raw[t], COPY, scale=gain_size[:, t : t + 1])

        w1_woven = keep.tile([P, PACK, P, PACK], BF16, name="w1_woven", align_bytes=64)
        w1_from = w1_raw[:].rearrange("p j (m t) -> p m j t", t=PACK)
        w1_to = w1_woven[:].rearrange("p t m j -> p m j t")
        nc.vector.tensor_copy(w1_to[:, 0:W1_ON_VECTOR], w1_from[:, 0:W1_ON_VECTOR])
        nc.scalar.copy(w1_to[:, W1_ON_VECTOR:P], w1_from[:, W1_ON_VECTOR:P])

        picked_bytes = keep.tile([P, S], U8, name="picked_bytes", align_bytes=64)
        nc.vector.tensor_copy(picked_bytes[:], x_bytes[:].indirect(offs_list[:]))

        w1_codes = keep.tile([P, H], U32, name="w1_codes", align_bytes=64)
        w1_bytes = keep.tile([P, H], U8, name="w1_bytes", align_bytes=64)
        nc.vector.quantize_mx(w1_codes[:].bitcast(FP8X4), w1_bytes[:], w1_woven[:].rearrange("p t m j -> p (t m j)"))

        picked_codes = keep.tile([P, S], U32, name="picked_codes", align_bytes=64)
        for lo, hi in HALVES:
            nc.vector.tensor_copy(picked_codes[:, lo:hi], x_codes[:].indirect(entries(offs_list, lo, hi)))

        tab_last_sized = keep.tile([P, J], F32, name="tab_last_sized", align_bytes=64)
        nc.vector.memset(hneg_win[LAST][:, S:], 0.0)
        nc.scalar.activation(tab_last_sized[:], tab_win[LAST][:], COPY, scale=gain_size[:, LAST : LAST + 1])
        for lo, hi in HALVES:
            nc.vector.tensor_copy(kind_sized[LAST][:, lo:hi], tab_last_sized[:].indirect(entries(n1_list, lo, hi)))

        def product(target, w_codes, w_bytes, block, v_codes, v_bytes, lo, hi):
            cols = slice(block * P, (block + 1) * P)
            nc.tensor.matmul_mx(
                out=target[:, lo:hi],
                lhsT=w_codes[:, cols].bitcast(FP8X4),
                lhsT_scale=w_bytes[:, cols],
                rhs=v_codes[:, lo:hi].bitcast(FP8X4),
                rhs_scale=v_bytes[:, lo:hi],
                start=True,
                stop=True,
            )

        bank = [psum.tile([P, S], F32, name=f"bank{b}") for b in range(BANKS)]
        st_win = planes("st_win", 2 * S)
        h_plain = [st_win[t][:, S:] for t in range(PACK)]
        with_kind = keep.tile([P, PACK, S], BF16, name="with_kind", align_bytes=64)
        y_fetched = keep.tile([P, PACK, S], BF16, name="y_fetched", align_bytes=64)
        for u, (lo, hi) in enumerate(HALVES):
            product(bank[u], w1_codes, w1_bytes, 0, picked_codes, picked_bytes, lo, hi)
            nc.scalar.activation(y_sized[0][:, lo:hi], bank[u][:, lo:hi], COPY, scale=gain_size[:, 0:1])
        for t in range(1, PACK):
            product(bank[t + 1], w1_codes, w1_bytes, t, picked_codes, picked_bytes, 0, S)
            nc.scalar.activation(y_sized[t], bank[t + 1][:], COPY, scale=gain_size[:, t : t + 1])

        w2_signed = keep.tile([P, PACK, N], BF16, name="w2_signed", tag="scratch16", align_bytes=64)
        for j in range(PACK):
            nc.scalar.activation(w2_signed[:, j, :], w2_raw[j // 2][:, j % 2, :], COPY, scale=gain_sign[:, j : j + 1])
        w2_woven = keep.tile([P, PACK, P, PACK], BF16, name="w2_woven", align_bytes=64)
        nc.scalar.copy(
            w2_woven[:].rearrange("p t m j -> p m j t"),
            w2_signed[:].rearrange("p j (m t) -> p m j t", t=PACK),
        )

        for t in range(PACK):
            for lo, hi in HALVES if t == 0 else [(0, S)]:
                nc.gpsimd.tensor_tensor(with_kind[:, t, lo:hi], kind_sized[t][:, lo:hi], y_sized[t][:, lo:hi], ALU.add)
            nc.vector.tensor_copy(y_fetched[:, t, :], y_win[t][:].indirect(n2_list[:]))

        larger = keep.tile([P, PACK, S], BF16, name="larger", tag=f"y_win{LAST}", align_bytes=64)
        z_woven = [
            keep.tile([P, S // 2, PACK], BF16, name="z_woven0", tag="scratch16", align_bytes=64),
            keep.tile([P, S // 2, PACK], BF16, name="z_woven1", align_bytes=64),
        ]
        for lo, hi in HALVES:
            nc.vector.tensor_tensor(larger[:, :, lo:hi], with_kind[:, :, lo:hi], y_fetched[:, :, lo:hi], ALU.max)

        def z_piece(u, lo, hi):
            return z_woven[u][:, lo - HALVES[u][0] : hi - HALVES[u][0], :]

        def weave_z(copy, u, lo, hi):
            copy(
                z_piece(u, lo, hi).rearrange("p (c i) t -> p c t i", i=RUN),
                larger[:, :, lo:hi].rearrange("p t (c i) -> p c t i", i=RUN),
            )

        for piece in Z_PIECES[1:]:
            weave_z(nc.scalar.copy, *piece)
        weave_z(nc.vector.tensor_copy, *Z_PIECES[0])

        def quantise_w2(u, **placed):
            codes = keep.tile([P, N // 2], U32, name=f"w2_codes{u}", align_bytes=64, **placed)
            scale_bytes = keep.tile([P, N // 2], U8, name=f"w2_bytes{u}", align_bytes=64)
            source = w2_woven[:, 2 * u : 2 * u + 2].rearrange("p t m j -> p (t m j)")
            nc.vector.quantize_mx(codes[:].bitcast(FP8X4), scale_bytes[:], source)
            return codes, scale_bytes

        w2_low = quantise_w2(0)

        z_codes = keep.tile([P, S], U32, name="z_codes", align_bytes=64)
        z_bytes = keep.tile([P, S], U8, name="z_bytes", align_bytes=64)
        piece_banks = bank[BANKS - len(Z_PIECES) :]
        for target, (u, lo, hi) in zip(piece_banks, Z_PIECES):
            nc.vector.quantize_mx(
                z_codes[:, lo:hi].bitcast(FP8X4), z_bytes[:, lo:hi], z_piece(u, lo, hi).rearrange("p n t -> p (n t)")
            )
            product(target, *w2_low, 0, z_codes, z_bytes, lo, hi)
            nc.scalar.activation(hneg_win[0][:, lo:hi], target[:, lo:hi], COPY, scale=-1.0)
            if u == 1:
                nc.scalar.copy(h_plain[0][:, lo:hi], target[:, lo:hi])
        for target, (u, lo, hi) in zip(piece_banks[1:], Z_PIECES[1:]):
            nc.scalar.copy(h_plain[0][:, lo:hi], target[:, lo:hi])
        w2_high = quantise_w2(1, tag="scratch16")
        for t in range(1, PACK):
            product(bank[t - 1], *(w2_low if t < 2 else w2_high), t % 2, z_codes, z_bytes, 0, S)
            nc.scalar.activation(hneg_win[t][:, :S], bank[t - 1][:], COPY, scale=-1.0)
            nc.scalar.copy(h_plain[t], bank[t - 1][:])

        identity = keep.tile([P, P], F32, name="identity")
        make_identity(nc, identity[:])
        st_fetched = planes("st_fetched", S)
        result = planes("result", S)
        st_turned = planes("st_turned", S, 2)
        excess_turned = planes("excess_turned", S, 2)
        out_rows = out.rearrange("(p t) c -> p t c", t=PACK)

        def make_st(t, lo, hi):
            nc.vector.tensor_tensor(
                st_win[t][:, lo:hi], hneg_win[t][:].indirect(entries(n3_list, lo, hi)), h_plain[t][:, lo:hi], ALU.add
            )

        def fetch_st(t, lo, hi):
            nc.vector.tensor_copy(st_fetched[t][:, lo:hi], st_win[t][:].indirect(entries(n4_list, lo, hi)))

        def finish_on_vector(t, lo, hi):
            nc.vector.tensor_tensor(result[t][:, lo:hi], st_win[t][:, lo:hi], st_fetched[t][:, lo:hi], ALU.max)
            nc.sync.dma_start(out_rows[:, t, lo:hi], result[t][:, lo:hi])

        def turn_sum(target, *terms):
            for block in range(S // P):
                cols = slice(block * P, (block + 1) * P)
                for i, term in enumerate(terms):
                    nc.tensor.matmul(
                        target[:, cols], term[:, cols], identity[:],
                        start=(i == 0), stop=(i == len(terms) - 1), is_transpose=True,
                    )

        def finish_by_relu(t, st_bank, diff_bank, out_bank):
            turn_sum(st_bank, st_win[t])
            nc.scalar.copy(st_turned[t][:], st_bank[:])
            nc.vector.tensor_scalar(st_fetched[t][:], st_win[t][:].indirect(n4_list[:]), -1.0, 0.0, ALU.mult, ALU.add)
            turn_sum(diff_bank, st_win[t], st_fetched[t])
            nc.scalar.activation(excess_turned[t][:], diff_bank[:], RELU, scale=-1.0)
            turn_sum(out_bank, st_turned[t], excess_turned[t])
            nc.scalar.copy(result[t][:], out_bank[:])
            nc.scalar.dma_start(out_rows[:, t, :], result[t][:])

        for lo, hi in reversed(HALVES):
            make_st(0, lo, hi)
        make_st(1, 0, S)
        finish_by_relu(0, bank[3], bank[4], bank[5])
        make_st(2, 0, S)
        finish_by_relu(1, bank[6], bank[7], bank[3])
        make_st(LAST, 0, S)
        fetch_st(2, 0, S)
        fetch_st(LAST, *HALVES[0])
        finish_on_vector(2, 0, S)
        fetch_st(LAST, *HALVES[1])
        for lo, hi in LAST_STORES:
            finish_on_vector(LAST, lo, hi)
